import numpy as np
CORES = [0,1,2,3,4,5,6,7]
N = 8
ROOT = 7
def setup_inputs(rng):
    return {"x": rng.standard_normal((N, 128, 4096), dtype=np.float32)}
def reference(x):
    y = np.full(x.shape, np.nan, x.dtype)
    y[ROOT] = x.sum(axis=0, dtype=np.float64).astype(x.dtype)
    return {"y": y}

@@ -1,0 +1,56 @@
+from concourse.bass import DstId, RemoteDMATransfer
+from concourse.mybir import AluOpType
+
+COLS = 4096
+NOWN = 7
+WMAX = -(-COLS // NOWN)
+
+SCRATCH = {
+    "full": ("sbuf", [128, COLS], "float32"),
+    "land": ("sbuf", [128, (NOWN - 1) * WMAX], "float32"),
+}
+SEMAPHORES = ["loaded", "sent", "arrived", "reduced"]
+
+
+def bounds(k):
+    base, extra = divmod(COLS, NOWN)
+    lo = k * base + min(k, extra)
+    return lo, lo + base + (1 if k < extra else 0)
+
+
+def rank_program(g, core, T, topo):
+    rank = T.rank_of(core)
+    if rank is None:
+        return
+    root = T.cores[T.root]
+    owners = [c for c in T.cores if c != root]
+
+    if core == root:
+        g.dma_start(T.y[:], T.x[:]).then_inc(T.sem.loaded, 16)
+        g.wait_ge(T.sem.loaded, 16)
+        g.wait_ge(T.sem.reduced, 16 * NOWN)
+        g.dma_start(T.y[:], T.full[:], accum_op=AluOpType.add, max_dma_last_dim=8192).then_inc(T.sem.loaded, 16)
+        g.wait_ge(T.sem.loaded, 32)
+        return
+
+    me = owners.index(core)
+    g.dma_start(T.full[:], T.x[:]).then_inc(T.sem.loaded, 16)
+    g.wait_ge(T.sem.loaded, 16)
+
+    for k, o in enumerate(owners):
+        if o == core:
+            continue
+        lo, hi = bounds(k)
+        slot = me if me < k else me - 1
+        rid, pid, _se = topo.addr(o)
+        g.remote_dma(T.land[:, slot * WMAX:slot * WMAX + hi - lo], T.full[:, lo:hi],
+                     T.sem.arrived, T.sem.sent, pid, rid, topo.mask(core, o))
+
+    g.wait_ge(T.sem.arrived, 16 * (NOWN - 1))
+    lo, hi = bounds(me)
+    rid, pid, _se = topo.addr(root)
+    srcs = [T.full[:, lo:hi]] + [T.land[:, s * WMAX:s * WMAX + hi - lo] for s in range(NOWN - 1)]
+    g.remote_dma_fused([RemoteDMATransfer(dst_ids=[DstId(rid=rid, pnc=pid)], dma_engine_mask=topo.mask(core, root),
+                                          remote_sem=T.sem.reduced, srcs=srcs, dsts=[T.full[:, lo:hi]], alu_op=1)],
+                       local_sem=T.sem.sent)
+    g.wait_ge(T.sem.sent, 16 * NOWN)

@@ -19,8 +19,7 @@ def bounds(k):
 
 
 def rank_program(g, core, T, topo):
-    rank = T.rank_of(core)
-    if rank is None:
+    if T.rank_of(core) is None:
         return
     root = T.cores[T.root]
     owners = [c for c in T.cores if c != root]
@@ -42,13 +41,13 @@ def rank_program(g, core, T, topo):
             continue
         lo, hi = bounds(k)
         slot = me if me < k else me - 1
-        rid, pid, _se = topo.addr(o)
+        rid, pid = topo.addr(o)[:2]
         g.remote_dma(T.land[:, slot * WMAX:slot * WMAX + hi - lo], T.full[:, lo:hi],
                      T.sem.arrived, T.sem.sent, pid, rid, topo.mask(core, o))
 
     g.wait_ge(T.sem.arrived, 16 * (NOWN - 1))
     lo, hi = bounds(me)
-    rid, pid, _se = topo.addr(root)
+    rid, pid = topo.addr(root)[:2]
     srcs = [T.full[:, lo:hi]] + [T.land[:, s * WMAX:s * WMAX + hi - lo] for s in range(NOWN - 1)]
     g.remote_dma_fused([RemoteDMATransfer(dst_ids=[DstId(rid=rid, pnc=pid)], dma_engine_mask=topo.mask(core, root),
                                           remote_sem=T.sem.reduced, srcs=srcs, dsts=[T.full[:, lo:hi]], alu_op=1)],

from concourse.bass import DstId, RemoteDMATransfer
from concourse.mybir import AluOpType

COLS = 4096
NOWN = 7
WMAX = -(-COLS // NOWN)

SCRATCH = {
    "full": ("sbuf", [128, COLS], "float32"),
    "land": ("sbuf", [128, (NOWN - 1) * WMAX], "float32"),
}
SEMAPHORES = ["loaded", "sent", "arrived", "reduced"]


def bounds(k):
    base, extra = divmod(COLS, NOWN)
    lo = k * base + min(k, extra)
    return lo, lo + base + (1 if k < extra else 0)


def rank_program(g, core, T, topo):
    if T.rank_of(core) is None:
        return
    root = T.cores[T.root]
    owners = [c for c in T.cores if c != root]

    if core == root:
        g.dma_start(T.y[:], T.x[:]).then_inc(T.sem.loaded, 16)
        g.wait_ge(T.sem.loaded, 16)
        g.wait_ge(T.sem.reduced, 16 * NOWN)
        g.dma_start(T.y[:], T.full[:], accum_op=AluOpType.add, max_dma_last_dim=8192).then_inc(T.sem.loaded, 16)
        g.wait_ge(T.sem.loaded, 32)
        return

    me = owners.index(core)
    g.dma_start(T.full[:], T.x[:]).then_inc(T.sem.loaded, 16)
    g.wait_ge(T.sem.loaded, 16)

    for k, o in enumerate(owners):
        if o == core:
            continue
        lo, hi = bounds(k)
        slot = me if me < k else me - 1
        rid, pid = topo.addr(o)[:2]
        g.remote_dma(T.land[:, slot * WMAX:slot * WMAX + hi - lo], T.full[:, lo:hi],
                     T.sem.arrived, T.sem.sent, pid, rid, topo.mask(core, o))

    g.wait_ge(T.sem.arrived, 16 * (NOWN - 1))
    lo, hi = bounds(me)
    rid, pid = topo.addr(root)[:2]
    srcs = [T.full[:, lo:hi]] + [T.land[:, s * WMAX:s * WMAX + hi - lo] for s in range(NOWN - 1)]
    g.remote_dma_fused([RemoteDMATransfer(dst_ids=[DstId(rid=rid, pnc=pid)], dma_engine_mask=topo.mask(core, root),
                                          remote_sem=T.sem.reduced, srcs=srcs, dsts=[T.full[:, lo:hi]], alu_op=1)],
                       local_sem=T.sem.sent)
    g.wait_ge(T.sem.sent, 16 * NOWN)
